import numpy as np
import ml_dtypes


def mxq(x, axis, fmt="e4m3"):
    dtype, down = {"e4m3": (ml_dtypes.float8_e4m3fn, 7), "e5m2": (ml_dtypes.float8_e5m2, 14)}[fmt]
    v = np.moveaxis(np.asarray(x, np.float32).astype(ml_dtypes.bfloat16).astype(np.float64), axis, -1)
    blocks = v.reshape(v.shape[:-1] + (-1, 32))
    amax = np.abs(blocks).max(-1, keepdims=True)
    byte = np.maximum(np.where(amax > 0, np.frexp(amax)[1] - 1 + 127, 0) - down, 1)
    scale = np.exp2(byte - 127.0)
    codes = (blocks / scale).astype(np.float32).astype(dtype).astype(np.float64)
    return np.moveaxis((codes * scale).reshape(v.shape), -1, axis)


WIDE = False


def mx_kscale(k):
    if not WIDE:
        return np.ones(k)
    levels = np.array([10, -10, 5, -5, 0])
    if k % 512:
        return np.exp2(np.random.permutation(np.resize(levels, k // 32))).repeat(32)
    a = np.empty((k // 512, 16))
    for p in range(k // 512):
        a[p, :8] = np.random.permutation(np.resize(levels, 8))
        for g in range(8):
            far = levels[np.abs(levels - a[p, g]) >= 10]
            a[p, g + 8] = far[np.random.randint(len(far))]
    return np.exp2(a.ravel()).repeat(32)


def f64(x):
    return np.asarray(x).astype(np.float64)


def striped(idx):
    return np.tile(idx.reshape(-1, 16).T, (8, 1)).astype(np.uint16)


def unstriped(offs):
    return offs[:16].T.reshape(-1).astype(np.int64)


def pack_weight(w):
    k, n = w.shape
    w = f64(np.asarray(w, np.float32).astype(ml_dtypes.bfloat16)).reshape(k // 32, 32, n)
    amax = np.abs(w).max(1)
    byte = np.clip(np.where(amax > 0, np.frexp(amax)[1] - 1 + 127 - 7, 1), 1, 254)
    scaled = (w * np.exp2(127.0 - byte)[:, None, :]).reshape(k, n).astype(np.float32)
    words = np.ascontiguousarray(scaled.reshape(k // 512, 128, 4, n).transpose(0, 1, 3, 2)).astype(ml_dtypes.float8_e4m3fn).view(np.uint8)
    return words, np.ascontiguousarray(byte.astype(np.uint8).reshape(k // 512, 16, n))


def unpack_weight(words, scales):
    g, p, n, _ = words.shape
    vals = np.ascontiguousarray(words).view(ml_dtypes.float8_e4m3fn).astype(np.float64) * np.repeat(np.exp2(scales.astype(np.float64) - 127.0), 8, axis=1)[..., None]
    return vals.transpose(0, 1, 3, 2).reshape(g * 512, n)


K, T, E, C, N = 2048, 512, 8, 128, 128


def by_expert(wq, xq):
    return np.concatenate([wq[e].T @ xq[:, e * C:(e + 1) * C] for e in range(E)], axis=1)


def setup_inputs():
    n = np.random.standard_normal
    s = mx_kscale(K)[:, None]
    first = np.random.permutation(np.repeat(np.arange(E), T // E))
    second = (first + 1 + np.random.permutation(np.repeat(np.arange(E - 1), -(-T // (E - 1)))[:T])) % E
    while np.bincount(second, minlength=E).max() != T // E:
        load = np.bincount(second, minlength=E); hi, lo = int(load.argmax()), int(load.argmin())
        t = np.flatnonzero((second == hi) & (first != lo))[0]; second[t] = lo
    slot_token = np.empty(E * C, np.int64); pos = np.empty((2, T), np.int64); fill = np.zeros(E, np.int64)
    place = np.stack([np.random.permutation(C) for _ in range(E)])
    for r, deal in enumerate((first, second)):
        for t in np.random.permutation(T):
            e = deal[t]; j = e * C + place[e, fill[e]]; fill[e] += 1; slot_token[j] = t; pos[r, t] = j
    g = np.random.uniform(0.2, 0.8, T)
    packed = [pack_weight(m) for m in n((E, K, N)) / np.sqrt(K) / s[None]]
    return {
        "xT": (n((K, T)) * s).astype(np.float32),
        "w_words": np.stack([m[0] for m in packed]),
        "w_scales": np.stack([m[1] for m in packed]),
        "b": (0.3 * n((N, E))).astype(np.float32),
        "gate": np.stack([np.tile(g, (N, 1)), np.tile(1.0 - g, (N, 1))]).astype(np.float32),
        "offs": striped(slot_token),
        "pos1": striped(pos[0]),
        "pos2": striped(pos[1]),
    }


def reference(xT, w_words, w_scales, b, gate, offs, pos1, pos2):
    idx = unstriped(offs)
    xq = mxq(f64(xT)[:, idx], 0, "e4m3")
    w = np.stack([unpack_weight(w_words[e], w_scales[e]) for e in range(E)])
    y = by_expert(w, xq)
    y = y + np.repeat(f64(b), C, axis=1)
    return f64(gate[0]) * y[:, unstriped(pos1)] + f64(gate[1]) * y[:, unstriped(pos2)]

@@ -1,0 +1,153 @@
+from contextlib import ExitStack
+
+import concourse.mybir as mybir
+
+K, T, E, C, N = 2048, 512, 8, 128, 128
+FLOPS = 2 * K * N * E * C
+
+F32 = mybir.dt.float32
+BF16 = mybir.dt.bfloat16
+I32 = mybir.dt.int32
+U32 = mybir.dt.uint32
+U16 = mybir.dt.uint16
+U8 = mybir.dt.uint8
+FP8X4 = mybir.dt.float8_e4m3fn_x4
+
+P = 128
+PACK = 4
+PASSES = K // (P * PACK)
+SLOTS = E * C
+HALF = T // 2
+WINDOW = 1408
+LAST_CUTS = ((0, 384), (384, 768), (768, 1024))
+
+
+def tile_routed_moe_kernel(tc, xT, w_words, w_scales, b, gate, offs, pos1, pos2, out):
+    nc = tc.nc
+    mult, add = mybir.AluOpType.mult, mybir.AluOpType.add
+    identity = mybir.ActivationFunctionType.Identity
+
+    with ExitStack() as ctx:
+        lists = ctx.enter_context(tc.tile_pool(name="lists", bufs=1))
+        keep = ctx.enter_context(tc.tile_pool(name="keep", bufs=1))
+        psum = ctx.enter_context(tc.psum_pool(name="psum", bufs=1))
+
+        offs_sb = lists.tile([P, SLOTS // 16], U16, name="offs_sb")
+        pos1_sb = lists.tile([P, T // 16], U16, name="pos1_sb")
+        pos2_sb = lists.tile([P, T // 16], U16, name="pos2_sb")
+
+        x_view = xT.rearrange("(g p j) t -> g p j t", p=P, j=PACK)
+        raw = [keep.tile([P, PACK, T], F32, name="raw%d" % g) for g in range(PASSES)]
+
+        def load_x(g, lo, hi):
+            nc.sync.dma_start(out=raw[g][:, :, lo:hi], in_=x_view[g][:, :, lo:hi])
+
+        w_planes = keep.tile([P, E * PASSES, N], U8, name="w_planes", align_bytes=64)
+        nc.gpsimd.memset(w_planes[:].rearrange("p c n -> p (c n)").bitcast(F32), 0.0)
+        x_planes = keep.tile([P, WINDOW], U8, name="x_planes", align_bytes=64)
+        nc.gpsimd.memset(x_planes[:, 0:T], 0)
+        x_codes = [keep.tile([P, WINDOW], I32, name="x_codes%d" % g, align_bytes=64) for g in range(PASSES)]
+
+        load_x(0, 0, HALF)
+        load_x(0, HALF, T)
+        nc.sync.dma_start(offs_sb[:], offs)
+        load_x(1, 0, HALF)
+        load_x(1, HALF, T)
+        load_x(2, 0, HALF)
+        load_x(2, HALF, T)
+        load_x(3, 0, HALF)
+        load_x(3, HALF, T)
+
+        s_view = w_scales.rearrange("e a (q r) n -> r q (e a) n", r=4)
+        for r in range(4):
+            nc.sync.dma_start(out=w_planes[r:P:32, :, :].bitcast(I32), in_=s_view[r].bitcast(I32))
+        b_sb = keep.tile([P, E], F32, name="b_sb")
+        nc.sync.dma_start(out=b_sb[:], in_=b)
+        nc.sync.dma_start(pos1_sb[:], pos1)
+        nc.sync.dma_start(pos2_sb[:], pos2)
+
+        w_view = w_words.rearrange("e a p n r -> p (e a) (n r)")
+        w_codes = [keep.tile([P, 2 * PASSES, N], I32, name="w_codes%d" % i, align_bytes=64) for i in range(E // 2)]
+        for i in range(E // 2):
+            nc.sync.dma_start(out=w_codes[i][:], in_=w_view[:, 2 * PASSES * i:2 * PASSES * (i + 1), :].bitcast(I32))
+
+        gate_sb = [keep.tile([P, T], F32, name="gate_sb%d" % r) for r in range(2)]
+        for r in range(2):
+            nc.sync.dma_start(out=gate_sb[r][:], in_=gate[r])
+
+        grouped = [keep.tile([P, T, PACK], BF16, name="grouped%d" % g, align_bytes=64) for g in range(PASSES)]
+        g_codes = [keep.tile([P, SLOTS], U32, name="g_codes%d" % g, align_bytes=64) for g in range(PASSES)]
+        g_planes = keep.tile([P, SLOTS], U8, name="g_planes", align_bytes=64)
+
+        def cast(engine_copy, g, lo, hi):
+            engine_copy(
+                out=grouped[g][:, lo:hi, :].rearrange("p (c i) j -> p c j i", i=4),
+                in_=raw[g][:, :, lo:hi].rearrange("p j (c i) -> p c j i", i=4),
+            )
+
+        def quantise(g, lo, hi):
+            nc.vector.quantize_mx(
+                out=x_codes[g][:, lo:hi].bitcast(FP8X4),
+                scales=x_planes[4 * g:P, lo:hi],
+                in_=grouped[g][:, lo:hi, :].rearrange("p t j -> p (t j)"),
+            )
+
+        def gather_codes(g, lo, hi):
+            nc.vector.tensor_copy(g_codes[g][:, lo:hi], x_codes[g][:].bitcast(U32).indirect(offs_sb[:, lo // 16:hi // 16]))
+
+        QUARTER = T // 4
+        cast(nc.vector.tensor_copy, 0, 0, QUARTER)
+        cast(nc.scalar.copy, 0, QUARTER, HALF)
+        quantise(0, 0, HALF)
+        cast(nc.vector.tensor_copy, 0, HALF, HALF + QUARTER)
+        cast(nc.scalar.copy, 0, HALF + QUARTER, T)
+        quantise(0, HALF, T)
+        for g in range(1, PASSES):
+            cast(nc.scalar.copy, g, 0, HALF)
+            cast(nc.scalar.copy, g, HALF, T)
+
+        gather_codes(0, 0, SLOTS)
+        quantise(1, 0, T)
+        gather_codes(1, 0, SLOTS)
+        quantise(2, 0, T)
+        gather_codes(2, 0, SLOTS)
+        quantise(3, 0, T)
+        nc.vector.tensor_copy(g_planes[:], x_planes[:].indirect(offs_sb[:]))
+        for lo, hi in LAST_CUTS:
+            gather_codes(PASSES - 1, lo, hi)
+
+        acc = [psum.tile([P, 512], F32, name="acc%d" % e) for e in range(E)]
+        y = keep.tile([P, SLOTS], F32, name="y")
+
+        def multiply(e, g):
+            cols = slice(e * C, (e + 1) * C)
+            nc.tensor.matmul_mx(
+                out=acc[e][:, 0:C],
+                lhsT=w_codes[e // 2][:, (e % 2) * PASSES + g, :].bitcast(FP8X4),
+                lhsT_scale=w_planes[:, e * PASSES + g, :],
+                rhs=g_codes[g][:, cols].bitcast(FP8X4),
+                rhs_scale=g_planes[4 * g:P, cols],
+                start=(g == 0),
+                stop=(g == PASSES - 1),
+            )
+
+        for e in range(E):
+            for g in range(PASSES - 1):
+                multiply(e, g)
+        for e in range(E):
+            multiply(e, PASSES - 1)
+            cols = slice(e * C, (e + 1) * C)
+            if e < E - 1:
+                nc.scalar.activation(out=y[:, cols], in_=acc[e][:, 0:C], func=identity, bias=b_sb[:, e:e + 1])
+            else:
+                nc.vector.tensor_scalar(out=y[:, cols], in0=acc[e][:, 0:C], scalar1=b_sb[:, e:e + 1], scalar2=None, op0=add)
+
+        part1 = keep.tile([P, T], F32, name="part1")
+        part2 = keep.tile([P, T], F32, name="part2")
+        total = keep.tile([P, T], F32, name="total")
+        nc.vector.tensor_tensor(part1[:], y[:].indirect(pos1_sb[:]), gate_sb[0][:], mult)
+        nc.vector.tensor_tensor(part2[:], y[:].indirect(pos2_sb[:]), gate_sb[1][:], mult)
+        nc.vector.tensor_tensor(total[:, 0:HALF], part1[:, 0:HALF], part2[:, 0:HALF], add)
+        nc.sync.dma_start(out=out[:, 0:HALF], in_=total[:, 0:HALF])
+        nc.vector.tensor_tensor(total[:, HALF:T], part1[:, HALF:T], part2[:, HALF:T], add)
+        nc.scalar.dma_start(out=out[:, HALF:T], in_=total[:, HALF:T])

@@ -19,7 +19,7 @@ PASSES = K // (P * PACK)
 SLOTS = E * C
 HALF = T // 2
 WINDOW = 1408
-LAST_CUTS = ((0, 384), (384, 768), (768, 1024))
+PAIR = 2 * C
 
 
 def tile_routed_moe_kernel(tc, xT, w_words, w_scales, b, gate, offs, pos1, pos2, out):
@@ -112,9 +112,15 @@ def tile_routed_moe_kernel(tc, xT, w_words, w_scales, b, gate, offs, pos1, pos2,
         quantise(2, 0, T)
         gather_codes(2, 0, SLOTS)
         quantise(3, 0, T)
-        nc.vector.tensor_copy(g_planes[:], x_planes[:].indirect(offs_sb[:]))
-        for lo, hi in LAST_CUTS:
-            gather_codes(PASSES - 1, lo, hi)
+
+        def gather_planes(lo, hi):
+            nc.vector.tensor_copy(g_planes[:, lo:hi], x_planes[:].indirect(offs_sb[:, lo // 16:hi // 16]))
+
+        gather_planes(0, PAIR)
+        for i in range(E // 2):
+            if i + 1 < E // 2:
+                gather_planes((i + 1) * PAIR, (i + 2) * PAIR)
+            gather_codes(PASSES - 1, i * PAIR, (i + 1) * PAIR)
 
         acc = [psum.tile([P, 512], F32, name="acc%d" % e) for e in range(E)]
         y = keep.tile([P, SLOTS], F32, name="y")
@@ -131,16 +137,17 @@ def tile_routed_moe_kernel(tc, xT, w_words, w_scales, b, gate, offs, pos1, pos2,
                 stop=(g == PASSES - 1),
             )
 
-        for e in range(E):
-            for g in range(PASSES - 1):
-                multiply(e, g)
-        for e in range(E):
-            multiply(e, PASSES - 1)
-            cols = slice(e * C, (e + 1) * C)
-            if e < E - 1:
-                nc.scalar.activation(out=y[:, cols], in_=acc[e][:, 0:C], func=identity, bias=b_sb[:, e:e + 1])
-            else:
-                nc.vector.tensor_scalar(out=y[:, cols], in0=acc[e][:, 0:C], scalar1=b_sb[:, e:e + 1], scalar2=None, op0=add)
+        for i in range(E // 2):
+            for e in (2 * i, 2 * i + 1):
+                for g in range(PASSES - 1):
+                    multiply(e, g)
+            for e in (2 * i, 2 * i + 1):
+                multiply(e, PASSES - 1)
+                cols = slice(e * C, (e + 1) * C)
+                if e < E - 1:
+                    nc.scalar.activation(out=y[:, cols], in_=acc[e][:, 0:C], func=identity, bias=b_sb[:, e:e + 1])
+                else:
+                    nc.vector.tensor_scalar(out=y[:, cols], in0=acc[e][:, 0:C], scalar1=b_sb[:, e:e + 1], scalar2=None, op0=add)
 
         part1 = keep.tile([P, T], F32, name="part1")
         part2 = keep.tile([P, T], F32, name="part2")

@@ -43,9 +43,9 @@ def tile_routed_moe_kernel(tc, xT, w_words, w_scales, b, gate, offs, pos1, pos2,
             nc.sync.dma_start(out=raw[g][:, :, lo:hi], in_=x_view[g][:, :, lo:hi])
 
         w_planes = keep.tile([P, E * PASSES, N], U8, name="w_planes", align_bytes=64)
-        nc.gpsimd.memset(w_planes[:].rearrange("p c n -> p (c n)").bitcast(F32), 0.0)
+        nc.vector.memset(w_planes[:].rearrange("p c n -> p (c n)").bitcast(I32), 0)
         x_planes = keep.tile([P, WINDOW], U8, name="x_planes", align_bytes=64)
-        nc.gpsimd.memset(x_planes[:, 0:T], 0)
+        nc.vector.memset(x_planes[:, 0:T].bitcast(I32), 0)
         x_codes = [keep.tile([P, WINDOW], I32, name="x_codes%d" % g, align_bytes=64) for g in range(PASSES)]
 
         load_x(0, 0, HALF)

@@ -55,21 +55,21 @@ def tile_routed_moe_kernel(tc, xT, w_words, w_scales, b, gate, offs, pos1, pos2,
         load_x(1, HALF, T)
         load_x(2, 0, HALF)
         load_x(2, HALF, T)
-        load_x(3, 0, HALF)
-        load_x(3, HALF, T)
+        load_x(3, 0, T)
 
         s_view = w_scales.rearrange("e a (q r) n -> r q (e a) n", r=4)
         for r in range(4):
             nc.sync.dma_start(out=w_planes[r:P:32, :, :].bitcast(I32), in_=s_view[r].bitcast(I32))
-        b_sb = keep.tile([P, E], F32, name="b_sb")
-        nc.sync.dma_start(out=b_sb[:], in_=b)
-        nc.sync.dma_start(pos1_sb[:], pos1)
-        nc.sync.dma_start(pos2_sb[:], pos2)
 
         w_view = w_words.rearrange("e a p n r -> p (e a) (n r)")
         w_codes = [keep.tile([P, 2 * PASSES, N], I32, name="w_codes%d" % i, align_bytes=64) for i in range(E // 2)]
         for i in range(E // 2):
             nc.sync.dma_start(out=w_codes[i][:], in_=w_view[:, 2 * PASSES * i:2 * PASSES * (i + 1), :].bitcast(I32))
+
+        b_sb = keep.tile([P, E], F32, name="b_sb")
+        nc.sync.dma_start(out=b_sb[:], in_=b)
+        nc.sync.dma_start(pos1_sb[:], pos1)
+        nc.sync.dma_start(pos2_sb[:], pos2)
 
         gate_sb = [keep.tile([P, T], F32, name="gate_sb%d" % r) for r in range(2)]
         for r in range(2):

@@ -19,6 +19,7 @@ PASSES = K // (P * PACK)
 SLOTS = E * C
 HALF = T // 2
 WINDOW = 1408
+LAST_WINDOW = 1024
 PAIR = 2 * C
 
 
@@ -46,7 +47,7 @@ def tile_routed_moe_kernel(tc, xT, w_words, w_scales, b, gate, offs, pos1, pos2,
         nc.vector.memset(w_planes[:].rearrange("p c n -> p (c n)").bitcast(I32), 0)
         x_planes = keep.tile([P, WINDOW], U8, name="x_planes", align_bytes=64)
         nc.vector.memset(x_planes[:, 0:T].bitcast(I32), 0)
-        x_codes = [keep.tile([P, WINDOW], I32, name="x_codes%d" % g, align_bytes=64) for g in range(PASSES)]
+        x_codes = [keep.tile([P, WINDOW if g < PASSES - 1 else LAST_WINDOW], I32, name="x_codes%d" % g, align_bytes=64) for g in range(PASSES)]
 
         load_x(0, 0, HALF)
         load_x(0, HALF, T)
@@ -85,6 +86,9 @@ def tile_routed_moe_kernel(tc, xT, w_words, w_scales, b, gate, offs, pos1, pos2,
                 in_=raw[g][:, :, lo:hi].rearrange("p j (c i) -> p c j i", i=4),
             )
 
+        def cast_in_turn(engine_copy, g, lo, hi):
+            engine_copy(out=grouped[g][:, lo:hi, :], in_=raw[g][:, :, lo:hi].rearrange("p j t -> p t j"))
+
         def quantise(g, lo, hi):
             nc.vector.quantize_mx(
                 out=x_codes[g][:, lo:hi].bitcast(FP8X4),
@@ -99,12 +103,16 @@ def tile_routed_moe_kernel(tc, xT, w_words, w_scales, b, gate, offs, pos1, pos2,
         cast(nc.vector.tensor_copy, 0, 0, QUARTER)
         cast(nc.scalar.copy, 0, QUARTER, HALF)
         quantise(0, 0, HALF)
-        cast(nc.vector.tensor_copy, 0, HALF, HALF + QUARTER)
-        cast(nc.scalar.copy, 0, HALF + QUARTER, T)
+        cast(nc.vector.tensor_copy, 0, HALF, T - QUARTER // 2)
+        cast(nc.scalar.copy, 0, T - QUARTER // 2, T)
         quantise(0, HALF, T)
         for g in range(1, PASSES):
             cast(nc.scalar.copy, g, 0, HALF)
-            cast(nc.scalar.copy, g, HALF, T)
+            if g == 1:
+                cast(nc.scalar.copy, g, HALF, T - QUARTER)
+                cast_in_turn(nc.gpsimd.tensor_copy, g, T - QUARTER, T)
+            else:
+                cast(nc.scalar.copy, g, HALF, T)
 
         gather_codes(0, 0, SLOTS)
         quantise(1, 0, T)
@@ -120,7 +128,10 @@ def tile_routed_moe_kernel(tc, xT, w_words, w_scales, b, gate, offs, pos1, pos2,
         for i in range(E // 2):
             if i + 1 < E // 2:
                 gather_planes((i + 1) * PAIR, (i + 2) * PAIR)
-            gather_codes(PASSES - 1, i * PAIR, (i + 1) * PAIR)
+            if i + 1 < E // 2:
+                gather_codes(PASSES - 1, i * PAIR, (i + 1) * PAIR)
+        for e in (E - 2, E - 1):
+            gather_codes(PASSES - 1, e * C, (e + 1) * C)
 
         acc = [psum.tile([P, 512], F32, name="acc%d" % e) for e in range(E)]
         y = keep.tile([P, SLOTS], F32, name="y")
@@ -153,8 +164,8 @@ def tile_routed_moe_kernel(tc, xT, w_words, w_scales, b, gate, offs, pos1, pos2,
         part2 = keep.tile([P, T], F32, name="part2")
         total = keep.tile([P, T], F32, name="total")
         nc.vector.tensor_tensor(part1[:], y[:].indirect(pos1_sb[:]), gate_sb[0][:], mult)
-        nc.vector.tensor_tensor(part2[:], y[:].indirect(pos2_sb[:]), gate_sb[1][:], mult)
-        nc.vector.tensor_tensor(total[:, 0:HALF], part1[:, 0:HALF], part2[:, 0:HALF], add)
-        nc.sync.dma_start(out=out[:, 0:HALF], in_=total[:, 0:HALF])
-        nc.vector.tensor_tensor(total[:, HALF:T], part1[:, HALF:T], part2[:, HALF:T], add)
-        nc.scalar.dma_start(out=out[:, HALF:T], in_=total[:, HALF:T])
+        for lo, hi, queue in ((0, T - QUARTER, nc.scalar), (T - QUARTER, T, nc.sync)):
+            cols = slice(lo, hi)
+            nc.vector.tensor_tensor(part2[:, cols], y[:].indirect(pos2_sb[:, lo // 16:hi // 16]), gate_sb[1][:, cols], mult)
+            nc.vector.tensor_tensor(total[:, cols], part1[:, cols], part2[:, cols], add)
+            queue.dma_start(out=out[:, cols], in_=total[:, cols])

@@ -49,14 +49,10 @@ def tile_routed_moe_kernel(tc, xT, w_words, w_scales, b, gate, offs, pos1, pos2,
         nc.vector.memset(x_planes[:, 0:T].bitcast(I32), 0)
         x_codes = [keep.tile([P, WINDOW if g < PASSES - 1 else LAST_WINDOW], I32, name="x_codes%d" % g, align_bytes=64) for g in range(PASSES)]
 
-        load_x(0, 0, HALF)
-        load_x(0, HALF, T)
+        load_x(0, 0, T)
         nc.sync.dma_start(offs_sb[:], offs)
-        load_x(1, 0, HALF)
-        load_x(1, HALF, T)
-        load_x(2, 0, HALF)
-        load_x(2, HALF, T)
-        load_x(3, 0, T)
+        for g in range(1, PASSES):
+            load_x(g, 0, T)
 
         s_view = w_scales.rearrange("e a (q r) n -> r q (e a) n", r=4)
         for r in range(4):
@@ -100,17 +96,16 @@ def tile_routed_moe_kernel(tc, xT, w_words, w_scales, b, gate, offs, pos1, pos2,
             nc.vector.tensor_copy(g_codes[g][:, lo:hi], x_codes[g][:].bitcast(U32).indirect(offs_sb[:, lo // 16:hi // 16]))
 
         QUARTER = T // 4
-        cast(nc.vector.tensor_copy, 0, 0, QUARTER)
-        cast(nc.scalar.copy, 0, QUARTER, HALF)
+        EIGHTH = T // 8
+        cast(nc.vector.tensor_copy, 0, 0, HALF)
+        cast(nc.scalar.copy, 0, HALF + EIGHTH, T)
         quantise(0, 0, HALF)
-        cast(nc.vector.tensor_copy, 0, HALF, T - QUARTER // 2)
-        cast(nc.scalar.copy, 0, T - QUARTER // 2, T)
+        cast(nc.vector.tensor_copy, 0, HALF, HALF + EIGHTH)
         quantise(0, HALF, T)
         for g in range(1, PASSES):
             cast(nc.scalar.copy, g, 0, HALF)
-            if g == 1:
-                cast(nc.scalar.copy, g, HALF, T - QUARTER)
-                cast_in_turn(nc.gpsimd.tensor_copy, g, T - QUARTER, T)
+            if g < PASSES - 1:
+                cast_in_turn(nc.gpsimd.tensor_copy, g, HALF, T)
             else:
                 cast(nc.scalar.copy, g, HALF, T)
 

@@ -38,7 +38,8 @@ def tile_routed_moe_kernel(tc, xT, w_words, w_scales, b, gate, offs, pos1, pos2,
         pos2_sb = lists.tile([P, T // 16], U16, name="pos2_sb")
 
         x_view = xT.rearrange("(g p j) t -> g p j t", p=P, j=PACK)
-        raw = [keep.tile([P, PACK, T], F32, name="raw%d" % g) for g in range(PASSES)]
+        turns = ctx.enter_context(tc.tile_pool(name="turns", bufs=1))
+        raw = [turns.tile([P, PACK, T], F32, name="raw%d" % g, tag="turn%d" % g, align_bytes=64) for g in range(PASSES)]
 
         def load_x(g, lo, hi):
             nc.sync.dma_start(out=raw[g][:, :, lo:hi], in_=x_view[g][:, :, lo:hi])
@@ -104,17 +105,17 @@ def tile_routed_moe_kernel(tc, xT, w_words, w_scales, b, gate, offs, pos1, pos2,
         quantise(0, HALF, T)
         for g in range(1, PASSES):
             cast(nc.scalar.copy, g, 0, HALF)
-            if g < PASSES - 1:
-                cast_in_turn(nc.gpsimd.tensor_copy, g, HALF, T)
-            else:
-                cast(nc.scalar.copy, g, HALF, T)
+            cast_in_turn(nc.gpsimd.tensor_copy, g, HALF, T)
 
         gather_codes(0, 0, SLOTS)
         quantise(1, 0, T)
-        gather_codes(1, 0, SLOTS)
-        quantise(2, 0, T)
-        gather_codes(2, 0, SLOTS)
-        quantise(3, 0, T)
+        LAST_PAIR = SLOTS - PAIR
+        last_pair_codes = {}
+        for g in (1, 2):
+            gather_codes(g, 0, LAST_PAIR)
+            quantise(g + 1, 0, T)
+            last_pair_codes[g] = turns.tile([P, PAIR], U32, name="last_pair_codes%d" % g, tag="turn%d" % (g + 1), align_bytes=64)
+            nc.vector.tensor_copy(last_pair_codes[g][:], x_codes[g][:].bitcast(U32).indirect(offs_sb[:, LAST_PAIR // 16:SLOTS // 16]))
 
         def gather_planes(lo, hi):
             nc.vector.tensor_copy(g_planes[:, lo:hi], x_planes[:].indirect(offs_sb[:, lo // 16:hi // 16]))
@@ -133,11 +134,15 @@ def tile_routed_moe_kernel(tc, xT, w_words, w_scales, b, gate, offs, pos1, pos2,
 
         def multiply(e, g):
             cols = slice(e * C, (e + 1) * C)
+            if g in last_pair_codes and e >= E - 2:
+                codes = last_pair_codes[g][:, e * C - LAST_PAIR:(e + 1) * C - LAST_PAIR]
+            else:
+                codes = g_codes[g][:, cols]
             nc.tensor.matmul_mx(
                 out=acc[e][:, 0:C],
                 lhsT=w_codes[e // 2][:, (e % 2) * PASSES + g, :].bitcast(FP8X4),
                 lhsT_scale=w_planes[:, e * PASSES + g, :],
-                rhs=g_codes[g][:, cols].bitcast(FP8X4),
+                rhs=codes.bitcast(FP8X4),
                 rhs_scale=g_planes[4 * g:P, cols],
                 start=(g == 0),
                 stop=(g == PASSES - 1),
@@ -159,8 +164,9 @@ def tile_routed_moe_kernel(tc, xT, w_words, w_scales, b, gate, offs, pos1, pos2,
         part2 = keep.tile([P, T], F32, name="part2")
         total = keep.tile([P, T], F32, name="total")
         nc.vector.tensor_tensor(part1[:], y[:].indirect(pos1_sb[:]), gate_sb[0][:], mult)
-        for lo, hi, queue in ((0, T - QUARTER, nc.scalar), (T - QUARTER, T, nc.sync)):
-            cols = slice(lo, hi)
-            nc.vector.tensor_tensor(part2[:, cols], y[:].indirect(pos2_sb[:, lo // 16:hi // 16]), gate_sb[1][:, cols], mult)
-            nc.vector.tensor_tensor(total[:, cols], part1[:, cols], part2[:, cols], add)
-            queue.dma_start(out=out[:, cols], in_=total[:, cols])
+        pieces = ((0, HALF, nc.scalar), (HALF, T, nc.sync))
+        for lo, hi, queue in pieces:
+            nc.vector.tensor_tensor(part2[:, lo:hi], y[:].indirect(pos2_sb[:, lo // 16:hi // 16]), gate_sb[1][:, lo:hi], mult)
+        for lo, hi, queue in pieces:
+            nc.vector.tensor_tensor(total[:, lo:hi], part1[:, lo:hi], part2[:, lo:hi], add)
+            queue.dma_start(out=out[:, lo:hi], in_=total[:, lo:hi])

@@ -52,17 +52,22 @@ def tile_routed_moe_kernel(tc, xT, w_words, w_scales, b, gate, offs, pos1, pos2,
 
         load_x(0, 0, T)
         nc.sync.dma_start(offs_sb[:], offs)
-        for g in range(1, PASSES):
+        for j in range(0, PACK, 2):
+            nc.sync.dma_start(out=raw[1][:, j:j + 2, :], in_=x_view[1][:, j:j + 2, :])
+        for g in range(2, PASSES):
             load_x(g, 0, T)
 
         s_view = w_scales.rearrange("e a (q r) n -> r q (e a) n", r=4)
         for r in range(4):
             nc.sync.dma_start(out=w_planes[r:P:32, :, :].bitcast(I32), in_=s_view[r].bitcast(I32))
 
-        w_view = w_words.rearrange("e a p n r -> p (e a) (n r)")
-        w_codes = [keep.tile([P, 2 * PASSES, N], I32, name="w_codes%d" % i, align_bytes=64) for i in range(E // 2)]
-        for i in range(E // 2):
-            nc.sync.dma_start(out=w_codes[i][:], in_=w_view[:, 2 * PASSES * i:2 * PASSES * (i + 1), :].bitcast(I32))
+        w_view = w_words.rearrange("e a p n r -> p e a (n r)")
+        w_codes = {}
+        for g, lo, hi in [(g, lo, lo + E // 2) for lo in (0, E // 2) for g in range(PASSES - 1)] + [(PASSES - 1, 0, E)]:
+            tile = keep.tile([P, hi - lo, N], I32, name="w_codes%d_%d" % (g, lo), align_bytes=64)
+            nc.sync.dma_start(out=tile[:], in_=w_view[:, lo:hi, g, :].bitcast(I32))
+            for e in range(lo, hi):
+                w_codes[e, g] = tile[:, e - lo, :]
 
         b_sb = keep.tile([P, E], F32, name="b_sb")
         nc.sync.dma_start(out=b_sb[:], in_=b)
@@ -77,14 +82,14 @@ def tile_routed_moe_kernel(tc, xT, w_words, w_scales, b, gate, offs, pos1, pos2,
         g_codes = [keep.tile([P, SLOTS], U32, name="g_codes%d" % g, align_bytes=64) for g in range(PASSES)]
         g_planes = keep.tile([P, SLOTS], U8, name="g_planes", align_bytes=64)
 
-        def cast(engine_copy, g, lo, hi):
+        def cast(engine_copy, g, lo, hi, j0=0, j1=PACK):
             engine_copy(
-                out=grouped[g][:, lo:hi, :].rearrange("p (c i) j -> p c j i", i=4),
-                in_=raw[g][:, :, lo:hi].rearrange("p j (c i) -> p c j i", i=4),
+                out=grouped[g][:, lo:hi, j0:j1].rearrange("p (c i) j -> p c j i", i=4),
+                in_=raw[g][:, j0:j1, lo:hi].rearrange("p j (c i) -> p c j i", i=4),
             )
 
-        def cast_in_turn(engine_copy, g, lo, hi):
-            engine_copy(out=grouped[g][:, lo:hi, :], in_=raw[g][:, :, lo:hi].rearrange("p j t -> p t j"))
+        def cast_in_turn(engine_copy, g, lo, hi, j0=0, j1=PACK):
+            engine_copy(out=grouped[g][:, lo:hi, j0:j1], in_=raw[g][:, j0:j1, lo:hi].rearrange("p j t -> p t j"))
 
         def quantise(g, lo, hi):
             nc.vector.quantize_mx(
@@ -100,12 +105,12 @@ def tile_routed_moe_kernel(tc, xT, w_words, w_scales, b, gate, offs, pos1, pos2,
         EIGHTH = T // 8
         cast(nc.vector.tensor_copy, 0, 0, HALF)
         cast(nc.scalar.copy, 0, HALF + EIGHTH, T)
-        quantise(0, 0, HALF)
         cast(nc.vector.tensor_copy, 0, HALF, HALF + EIGHTH)
+        quantise(0, 0, HALF)
         quantise(0, HALF, T)
-        for g in range(1, PASSES):
-            cast(nc.scalar.copy, g, 0, HALF)
-            cast_in_turn(nc.gpsimd.tensor_copy, g, HALF, T)
+        for g, j0, j1 in ((1, 0, 2), (1, 2, PACK), (2, 0, PACK), (3, 0, PACK)):
+            cast(nc.scalar.copy, g, 0, HALF, j0, j1)
+            cast_in_turn(nc.gpsimd.tensor_copy, g, HALF, T, j0, j1)
 
         gather_codes(0, 0, SLOTS)
         quantise(1, 0, T)
@@ -120,14 +125,10 @@ def tile_routed_moe_kernel(tc, xT, w_words, w_scales, b, gate, offs, pos1, pos2,
         def gather_planes(lo, hi):
             nc.vector.tensor_copy(g_planes[:, lo:hi], x_planes[:].indirect(offs_sb[:, lo // 16:hi // 16]))
 
-        gather_planes(0, PAIR)
-        for i in range(E // 2):
-            if i + 1 < E // 2:
-                gather_planes((i + 1) * PAIR, (i + 2) * PAIR)
-            if i + 1 < E // 2:
-                gather_codes(PASSES - 1, i * PAIR, (i + 1) * PAIR)
-        for e in (E - 2, E - 1):
-            gather_codes(PASSES - 1, e * C, (e + 1) * C)
+        for lo, hi in ((0, 2), (2, 4), (4, E)):
+            gather_planes(lo * C, hi * C)
+        for lo, hi in ((0, 4), (4, E - 1), (E - 1, E)):
+            gather_codes(PASSES - 1, lo * C, hi * C)
 
         acc = [psum.tile([P, 512], F32, name="acc%d" % e) for e in range(E)]
         y = keep.tile([P, SLOTS], F32, name="y")
@@ -140,7 +141,7 @@ def tile_routed_moe_kernel(tc, xT, w_words, w_scales, b, gate, offs, pos1, pos2,
                 codes = g_codes[g][:, cols]
             nc.tensor.matmul_mx(
                 out=acc[e][:, 0:C],
-                lhsT=w_codes[e // 2][:, (e % 2) * PASSES + g, :].bitcast(FP8X4),
+                lhsT=w_codes[e, g].bitcast(FP8X4),
                 lhsT_scale=w_planes[:, e * PASSES + g, :],
                 rhs=codes.bitcast(FP8X4),
                 rhs_scale=g_planes[4 * g:P, cols],
@@ -148,17 +149,17 @@ def tile_routed_moe_kernel(tc, xT, w_words, w_scales, b, gate, offs, pos1, pos2,
                 stop=(g == PASSES - 1),
             )
 
-        for i in range(E // 2):
-            for e in (2 * i, 2 * i + 1):
-                for g in range(PASSES - 1):
+        for lo in (0, E // 2):
+            for g in range(PASSES - 1):
+                for e in range(lo, lo + E // 2):
                     multiply(e, g)
-            for e in (2 * i, 2 * i + 1):
-                multiply(e, PASSES - 1)
-                cols = slice(e * C, (e + 1) * C)
-                if e < E - 1:
-                    nc.scalar.activation(out=y[:, cols], in_=acc[e][:, 0:C], func=identity, bias=b_sb[:, e:e + 1])
-                else:
-                    nc.vector.tensor_scalar(out=y[:, cols], in0=acc[e][:, 0:C], scalar1=b_sb[:, e:e + 1], scalar2=None, op0=add)
+        for e in range(E):
+            multiply(e, PASSES - 1)
+            cols = slice(e * C, (e + 1) * C)
+            if e < E - 1:
+                nc.scalar.activation(out=y[:, cols], in_=acc[e][:, 0:C], func=identity, bias=b_sb[:, e:e + 1])
+            else:
+                nc.vector.tensor_scalar(out=y[:, cols], in0=acc[e][:, 0:C], scalar1=b_sb[:, e:e + 1], scalar2=None, op0=add)
 
         part1 = keep.tile([P, T], F32, name="part1")
         part2 = keep.tile([P, T], F32, name="part2")

@@ -52,10 +52,11 @@ def tile_routed_moe_kernel(tc, xT, w_words, w_scales, b, gate, offs, pos1, pos2,
 
         load_x(0, 0, T)
         nc.sync.dma_start(offs_sb[:], offs)
-        for j in range(0, PACK, 2):
-            nc.sync.dma_start(out=raw[1][:, j:j + 2, :], in_=x_view[1][:, j:j + 2, :])
-        for g in range(2, PASSES):
+        for g in range(1, PASSES):
             load_x(g, 0, T)
+
+        b_sb = keep.tile([P, E], F32, name="b_sb")
+        nc.sync.dma_start(out=b_sb[:], in_=b)
 
         s_view = w_scales.rearrange("e a (q r) n -> r q (e a) n", r=4)
         for r in range(4):
@@ -63,33 +64,29 @@ def tile_routed_moe_kernel(tc, xT, w_words, w_scales, b, gate, offs, pos1, pos2,
 
         w_view = w_words.rearrange("e a p n r -> p e a (n r)")
         w_codes = {}
-        for g, lo, hi in [(g, lo, lo + E // 2) for lo in (0, E // 2) for g in range(PASSES - 1)] + [(PASSES - 1, 0, E)]:
+        for g, lo, hi in [(g, lo, lo + E // 2) for lo in (0, E // 2) for g in range(PASSES - 1)] + [(PASSES - 1, lo, lo + E // 2) for lo in (0, E // 2)]:
             tile = keep.tile([P, hi - lo, N], I32, name="w_codes%d_%d" % (g, lo), align_bytes=64)
             nc.sync.dma_start(out=tile[:], in_=w_view[:, lo:hi, g, :].bitcast(I32))
             for e in range(lo, hi):
                 w_codes[e, g] = tile[:, e - lo, :]
 
-        b_sb = keep.tile([P, E], F32, name="b_sb")
-        nc.sync.dma_start(out=b_sb[:], in_=b)
-        nc.sync.dma_start(pos1_sb[:], pos1)
-        nc.sync.dma_start(pos2_sb[:], pos2)
-
         gate_sb = [keep.tile([P, T], F32, name="gate_sb%d" % r) for r in range(2)]
-        for r in range(2):
+        for r, (pos_sb, pos) in enumerate(((pos1_sb, pos1), (pos2_sb, pos2))):
+            nc.sync.dma_start(pos_sb[:], pos)
             nc.sync.dma_start(out=gate_sb[r][:], in_=gate[r])
 
         grouped = [keep.tile([P, T, PACK], BF16, name="grouped%d" % g, align_bytes=64) for g in range(PASSES)]
         g_codes = [keep.tile([P, SLOTS], U32, name="g_codes%d" % g, align_bytes=64) for g in range(PASSES)]
         g_planes = keep.tile([P, SLOTS], U8, name="g_planes", align_bytes=64)
 
-        def cast(engine_copy, g, lo, hi, j0=0, j1=PACK):
+        def cast(engine_copy, g, lo, hi):
             engine_copy(
-                out=grouped[g][:, lo:hi, j0:j1].rearrange("p (c i) j -> p c j i", i=4),
-                in_=raw[g][:, j0:j1, lo:hi].rearrange("p j (c i) -> p c j i", i=4),
+                out=grouped[g][:, lo:hi, :].rearrange("p (c i) j -> p c j i", i=4),
+                in_=raw[g][:, :, lo:hi].rearrange("p j (c i) -> p c j i", i=4),
             )
 
-        def cast_in_turn(engine_copy, g, lo, hi, j0=0, j1=PACK):
-            engine_copy(out=grouped[g][:, lo:hi, j0:j1], in_=raw[g][:, j0:j1, lo:hi].rearrange("p j t -> p t j"))
+        def cast_in_turn(engine_copy, g, lo, hi):
+            engine_copy(out=grouped[g][:, lo:hi, :], in_=raw[g][:, :, lo:hi].rearrange("p j t -> p t j"))
 
         def quantise(g, lo, hi):
             nc.vector.quantize_mx(
@@ -108,9 +105,9 @@ def tile_routed_moe_kernel(tc, xT, w_words, w_scales, b, gate, offs, pos1, pos2,
         cast(nc.vector.tensor_copy, 0, HALF, HALF + EIGHTH)
         quantise(0, 0, HALF)
         quantise(0, HALF, T)
-        for g, j0, j1 in ((1, 0, 2), (1, 2, PACK), (2, 0, PACK), (3, 0, PACK)):
-            cast(nc.scalar.copy, g, 0, HALF, j0, j1)
-            cast_in_turn(nc.gpsimd.tensor_copy, g, HALF, T, j0, j1)
+        for g in range(1, PASSES):
+            cast(nc.scalar.copy, g, 0, HALF)
+            cast_in_turn(nc.gpsimd.tensor_copy, g, HALF, T)
 
         gather_codes(0, 0, SLOTS)
         quantise(1, 0, T)
@@ -156,7 +153,7 @@ def tile_routed_moe_kernel(tc, xT, w_words, w_scales, b, gate, offs, pos1, pos2,
         for e in range(E):
             multiply(e, PASSES - 1)
             cols = slice(e * C, (e + 1) * C)
-            if e < E - 1:
+            if e != E - 2:
                 nc.scalar.activation(out=y[:, cols], in_=acc[e][:, 0:C], func=identity, bias=b_sb[:, e:e + 1])
             else:
                 nc.vector.tensor_scalar(out=y[:, cols], in0=acc[e][:, 0:C], scalar1=b_sb[:, e:e + 1], scalar2=None, op0=add)

@@ -105,9 +105,10 @@ def tile_routed_moe_kernel(tc, xT, w_words, w_scales, b, gate, offs, pos1, pos2,
         cast(nc.vector.tensor_copy, 0, HALF, HALF + EIGHTH)
         quantise(0, 0, HALF)
         quantise(0, HALF, T)
+        SHARE = HALF + T // 16
         for g in range(1, PASSES):
-            cast(nc.scalar.copy, g, 0, HALF)
-            cast_in_turn(nc.gpsimd.tensor_copy, g, HALF, T)
+            cast(nc.scalar.copy, g, 0, SHARE)
+            cast_in_turn(nc.gpsimd.tensor_copy, g, SHARE, T)
 
         gather_codes(0, 0, SLOTS)
         quantise(1, 0, T)

from contextlib import ExitStack

import concourse.mybir as mybir

K, T, E, C, N = 2048, 512, 8, 128, 128
FLOPS = 2 * K * N * E * C

F32 = mybir.dt.float32
BF16 = mybir.dt.bfloat16
I32 = mybir.dt.int32
U32 = mybir.dt.uint32
U16 = mybir.dt.uint16
U8 = mybir.dt.uint8
FP8X4 = mybir.dt.float8_e4m3fn_x4

P = 128
PACK = 4
PASSES = K // (P * PACK)
SLOTS = E * C
HALF = T // 2
WINDOW = 1408
LAST_WINDOW = 1024
PAIR = 2 * C


def tile_routed_moe_kernel(tc, xT, w_words, w_scales, b, gate, offs, pos1, pos2, out):
    nc = tc.nc
    mult, add = mybir.AluOpType.mult, mybir.AluOpType.add
    identity = mybir.ActivationFunctionType.Identity

    with ExitStack() as ctx:
        lists = ctx.enter_context(tc.tile_pool(name="lists", bufs=1))
        keep = ctx.enter_context(tc.tile_pool(name="keep", bufs=1))
        psum = ctx.enter_context(tc.psum_pool(name="psum", bufs=1))

        offs_sb = lists.tile([P, SLOTS // 16], U16, name="offs_sb")
        pos1_sb = lists.tile([P, T // 16], U16, name="pos1_sb")
        pos2_sb = lists.tile([P, T // 16], U16, name="pos2_sb")

        x_view = xT.rearrange("(g p j) t -> g p j t", p=P, j=PACK)
        turns = ctx.enter_context(tc.tile_pool(name="turns", bufs=1))
        raw = [turns.tile([P, PACK, T], F32, name="raw%d" % g, tag="turn%d" % g, align_bytes=64) for g in range(PASSES)]

        def load_x(g, lo, hi):
            nc.sync.dma_start(out=raw[g][:, :, lo:hi], in_=x_view[g][:, :, lo:hi])

        w_planes = keep.tile([P, E * PASSES, N], U8, name="w_planes", align_bytes=64)
        nc.vector.memset(w_planes[:].rearrange("p c n -> p (c n)").bitcast(I32), 0)
        x_planes = keep.tile([P, WINDOW], U8, name="x_planes", align_bytes=64)
        nc.vector.memset(x_planes[:, 0:T].bitcast(I32), 0)
        x_codes = [keep.tile([P, WINDOW if g < PASSES - 1 else LAST_WINDOW], I32, name="x_codes%d" % g, align_bytes=64) for g in range(PASSES)]

        load_x(0, 0, T)
        nc.sync.dma_start(offs_sb[:], offs)
        for g in range(1, PASSES):
            load_x(g, 0, T)

        b_sb = keep.tile([P, E], F32, name="b_sb")
        nc.sync.dma_start(out=b_sb[:], in_=b)

        s_view = w_scales.rearrange("e a (q r) n -> r q (e a) n", r=4)
        for r in range(4):
            nc.sync.dma_start(out=w_planes[r:P:32, :, :].bitcast(I32), in_=s_view[r].bitcast(I32))

        w_view = w_words.rearrange("e a p n r -> p e a (n r)")
        w_codes = {}
        for g, lo, hi in [(g, lo, lo + E // 2) for lo in (0, E // 2) for g in range(PASSES - 1)] + [(PASSES - 1, lo, lo + E // 2) for lo in (0, E // 2)]:
            tile = keep.tile([P, hi - lo, N], I32, name="w_codes%d_%d" % (g, lo), align_bytes=64)
            nc.sync.dma_start(out=tile[:], in_=w_view[:, lo:hi, g, :].bitcast(I32))
            for e in range(lo, hi):
                w_codes[e, g] = tile[:, e - lo, :]

        gate_sb = [keep.tile([P, T], F32, name="gate_sb%d" % r) for r in range(2)]
        for r, (pos_sb, pos) in enumerate(((pos1_sb, pos1), (pos2_sb, pos2))):
            nc.sync.dma_start(pos_sb[:], pos)
            nc.sync.dma_start(out=gate_sb[r][:], in_=gate[r])

        grouped = [keep.tile([P, T, PACK], BF16, name="grouped%d" % g, align_bytes=64) for g in range(PASSES)]
        g_codes = [keep.tile([P, SLOTS], U32, name="g_codes%d" % g, align_bytes=64) for g in range(PASSES)]
        g_planes = keep.tile([P, SLOTS], U8, name="g_planes", align_bytes=64)

        def cast(engine_copy, g, lo, hi):
            engine_copy(
                out=grouped[g][:, lo:hi, :].rearrange("p (c i) j -> p c j i", i=4),
                in_=raw[g][:, :, lo:hi].rearrange("p j (c i) -> p c j i", i=4),
            )

        def cast_in_turn(engine_copy, g, lo, hi):
            engine_copy(out=grouped[g][:, lo:hi, :], in_=raw[g][:, :, lo:hi].rearrange("p j t -> p t j"))

        def quantise(g, lo, hi):
            nc.vector.quantize_mx(
                out=x_codes[g][:, lo:hi].bitcast(FP8X4),
                scales=x_planes[4 * g:P, lo:hi],
                in_=grouped[g][:, lo:hi, :].rearrange("p t j -> p (t j)"),
            )

        def gather_codes(g, lo, hi):
            nc.vector.tensor_copy(g_codes[g][:, lo:hi], x_codes[g][:].bitcast(U32).indirect(offs_sb[:, lo // 16:hi // 16]))

        QUARTER = T // 4
        EIGHTH = T // 8
        cast(nc.vector.tensor_copy, 0, 0, HALF)
        cast(nc.scalar.copy, 0, HALF + EIGHTH, T)
        cast(nc.vector.tensor_copy, 0, HALF, HALF + EIGHTH)
        quantise(0, 0, HALF)
        quantise(0, HALF, T)
        SHARE = HALF + T // 16
        for g in range(1, PASSES):
            cast(nc.scalar.copy, g, 0, SHARE)
            cast_in_turn(nc.gpsimd.tensor_copy, g, SHARE, T)

        gather_codes(0, 0, SLOTS)
        quantise(1, 0, T)
        LAST_PAIR = SLOTS - PAIR
        last_pair_codes = {}
        for g in (1, 2):
            gather_codes(g, 0, LAST_PAIR)
            quantise(g + 1, 0, T)
            last_pair_codes[g] = turns.tile([P, PAIR], U32, name="last_pair_codes%d" % g, tag="turn%d" % (g + 1), align_bytes=64)
            nc.vector.tensor_copy(last_pair_codes[g][:], x_codes[g][:].bitcast(U32).indirect(offs_sb[:, LAST_PAIR // 16:SLOTS // 16]))

        def gather_planes(lo, hi):
            nc.vector.tensor_copy(g_planes[:, lo:hi], x_planes[:].indirect(offs_sb[:, lo // 16:hi // 16]))

        for lo, hi in ((0, 2), (2, 4), (4, E)):
            gather_planes(lo * C, hi * C)
        for lo, hi in ((0, 4), (4, E - 1), (E - 1, E)):
            gather_codes(PASSES - 1, lo * C, hi * C)

        acc = [psum.tile([P, 512], F32, name="acc%d" % e) for e in range(E)]
        y = keep.tile([P, SLOTS], F32, name="y")

        def multiply(e, g):
            cols = slice(e * C, (e + 1) * C)
            if g in last_pair_codes and e >= E - 2:
                codes = last_pair_codes[g][:, e * C - LAST_PAIR:(e + 1) * C - LAST_PAIR]
            else:
                codes = g_codes[g][:, cols]
            nc.tensor.matmul_mx(
                out=acc[e][:, 0:C],
                lhsT=w_codes[e, g].bitcast(FP8X4),
                lhsT_scale=w_planes[:, e * PASSES + g, :],
                rhs=codes.bitcast(FP8X4),
                rhs_scale=g_planes[4 * g:P, cols],
                start=(g == 0),
                stop=(g == PASSES - 1),
            )

        for lo in (0, E // 2):
            for g in range(PASSES - 1):
                for e in range(lo, lo + E // 2):
                    multiply(e, g)
        for e in range(E):
            multiply(e, PASSES - 1)
            cols = slice(e * C, (e + 1) * C)
            if e != E - 2:
                nc.scalar.activation(out=y[:, cols], in_=acc[e][:, 0:C], func=identity, bias=b_sb[:, e:e + 1])
            else:
                nc.vector.tensor_scalar(out=y[:, cols], in0=acc[e][:, 0:C], scalar1=b_sb[:, e:e + 1], scalar2=None, op0=add)

        part1 = keep.tile([P, T], F32, name="part1")
        part2 = keep.tile([P, T], F32, name="part2")
        total = keep.tile([P, T], F32, name="total")
        nc.vector.tensor_tensor(part1[:], y[:].indirect(pos1_sb[:]), gate_sb[0][:], mult)
        pieces = ((0, HALF, nc.scalar), (HALF, T, nc.sync))
        for lo, hi, queue in pieces:
            nc.vector.tensor_tensor(part2[:, lo:hi], y[:].indirect(pos2_sb[:, lo // 16:hi // 16]), gate_sb[1][:, lo:hi], mult)
        for lo, hi, queue in pieces:
            nc.vector.tensor_tensor(total[:, lo:hi], part1[:, lo:hi], part2[:, lo:hi], add)
            queue.dma_start(out=out[:, lo:hi], in_=total[:, lo:hi])
